import numpy as np
import ml_dtypes


def mxq(x, axis, fmt="e4m3"):
    dtype, down = {"e4m3": (ml_dtypes.float8_e4m3fn, 7), "e5m2": (ml_dtypes.float8_e5m2, 14)}[fmt]
    v = np.moveaxis(np.asarray(x, np.float32).astype(ml_dtypes.bfloat16).astype(np.float64), axis, -1)
    blocks = v.reshape(v.shape[:-1] + (-1, 32))
    amax = np.abs(blocks).max(-1, keepdims=True)
    byte = np.maximum(np.where(amax > 0, np.frexp(amax)[1] - 1 + 127, 0) - down, 1)
    scale = np.exp2(byte - 127.0)
    codes = (blocks / scale).astype(np.float32).astype(dtype).astype(np.float64)
    return np.moveaxis((codes * scale).reshape(v.shape), -1, axis)


WIDE = False


def mx_kscale(k):
    if not WIDE:
        return np.ones(k)
    levels = np.array([30, -30])
    if k % 512:
        return np.exp2(np.random.permutation(np.resize(levels, k // 32))).repeat(32)
    a = np.empty((k // 512, 16))
    for p in range(k // 512):
        a[p, :8] = np.random.permutation(np.resize(levels, 8))
        for g in range(8):
            far = levels[np.abs(levels - a[p, g]) >= 10]
            a[p, g + 8] = far[np.random.randint(len(far))]
    return np.exp2(a.ravel()).repeat(32)


def f64(x):
    return np.asarray(x).astype(np.float64)


def striped(idx):
    return np.tile(np.asarray(idx).reshape(-1, 16).T, (8, 1)).astype(np.uint16)


def unstriped(offs):
    return offs[:16].T.reshape(-1).astype(np.int64)


E2M1 = np.array([0.0, 0.5, 1.0, 1.5, 2.0, 3.0, 4.0, 6.0, -0.0, -0.5, -1.0, -1.5, -2.0, -3.0, -4.0, -6.0])


def pack_weight(w, fmt):
    k, n = w.shape
    w = f64(np.asarray(w, np.float32).astype(ml_dtypes.bfloat16)).reshape(k // 32, 32, n)
    amax = np.abs(w).max(1)
    if fmt == "e4m3":
        byte = np.frexp(amax)[1] - 1 + 127 - 7
    else:
        mant, ex = np.frexp(amax / 6.0)
        byte = np.where(mant > 0.5, ex, ex - 1) + 127
    byte = np.clip(np.where(amax > 0, byte, 1), 1, 254)
    scaled = (w * np.exp2(127.0 - byte)[:, None, :]).reshape(k, n).astype(np.float32)
    by_word = np.ascontiguousarray(scaled.reshape(k // 512, 128, 4, n).transpose(0, 1, 3, 2))
    if fmt == "e4m3":
        words = by_word.astype(ml_dtypes.float8_e4m3fn).view(np.uint8)
    else:
        c = by_word.astype(ml_dtypes.float4_e2m1fn).view(np.uint8) & 0xF
        words = (c[..., 0::2] | (c[..., 1::2] << 4)).reshape(k // 512, 128, 2 * n)
    return np.ascontiguousarray(words), np.ascontiguousarray(byte.astype(np.uint8).reshape(k // 512, 16, n))


def unpack_weight(words, scales, fmt):
    g, _, n = scales.shape
    words = np.ascontiguousarray(words).reshape(g, 128, n, -1)
    if fmt == "e4m3":
        vals = words.view(ml_dtypes.float8_e4m3fn).astype(np.float64)
    else:
        nib = np.empty((g, 128, n, 4), np.uint8)
        nib[..., 0::2] = words & 0xF
        nib[..., 1::2] = words >> 4
        vals = E2M1[nib]
    vals = vals * np.repeat(np.exp2(scales.astype(np.float64) - 127.0), 8, axis=1)[..., None]
    return vals.transpose(0, 1, 3, 2).reshape(g * 512, n)


def sigmoid(v):
    return 1.0 / (1.0 + np.exp(-v))


K, T, J, R, C, N = 512, 512, 256, 512, 1024, 256


def setup_inputs():
    n = np.random.standard_normal
    idx = np.random.permutation(T)[:J]
    idx2 = np.random.permutation(T)[:J]
    idx3 = np.random.permutation(C)[:R]
    fk = mx_kscale(K)
    fr = mx_kscale(R)
    wp = pack_weight(n((K, R)) * 1 / np.sqrt(K) * fk[:, None], "e2m1")
    wbp = pack_weight(n((R, N)) * 1 / np.sqrt(R) / fr[:, None], "e2m1")
    return {
        "xf": (n((K, T))).astype(np.float32),
        "fk": (np.random.uniform(0.5, 2.0, (K, 1)) / fk[:, None]).astype(np.float32),
        "w_words": wp[0],
        "w_scales": wp[1],
        "us": (np.random.uniform(0.5, 1.5, (1, R)) * fr).astype(np.float32),
        "tg": (1.0 * n((J, C))).astype(np.float32),
        "wb_words": wbp[0],
        "wb_scales": wbp[1],
        "rs": (1.0 * n((J, N))).astype(np.float32),
        "offs": striped(idx),
        "offs2": striped(idx2),
        "offs3": striped(idx3),
    }


def reference(xf, fk, w_words, w_scales, us, tg, wb_words, wb_scales, rs, offs, offs2, offs3):
    idx = unstriped(offs)
    idx2 = unstriped(offs2)
    idx3 = unstriped(offs3)
    wu = unpack_weight(w_words, w_scales, "e2m1")
    wbu = unpack_weight(wb_words, wb_scales, "e2m1")
    u = np.maximum(f64(xf)[:, idx], f64(xf)[:, idx2]) * f64(fk)
    uq = mxq(u, 0, "e4m3")
    a = uq.T @ wu
    hr = a * sigmoid(f64(tg)[:, idx3]) * f64(us)
    hid = hr.T
    hidq = mxq(hid, 0, "e5m2")
    p = hidq.T @ wbu
    pk2 = np.max(np.abs(p), axis=1, keepdims=True)
    y = p / (pk2 + 0.2) + 0.3 * f64(rs)
    return y

@@ -1,0 +1,195 @@
+from contextlib import ExitStack
+
+import concourse.mybir as mybir
+from concourse.masks import make_identity
+
+K, T, J, R, C, N = 512, 512, 256, 512, 1024, 256
+FLOPS = 2 * K * J * R + 2 * R * J * N
+
+F32 = mybir.dt.float32
+BF16 = mybir.dt.bfloat16
+I32 = mybir.dt.int32
+U32 = mybir.dt.uint32
+U16 = mybir.dt.uint16
+U8 = mybir.dt.uint8
+E4M3 = mybir.dt.float8_e4m3fn_x4
+E5M2 = mybir.dt.float8_e5m2_x4
+E2M1 = mybir.dt.float4_e2m1fn_x4
+ALU = mybir.AluOpType
+ACT = mybir.ActivationFunctionType
+
+P = 128
+PACK = 4
+HALVES = J // P
+RUN = 4
+
+
+def load_scale_rows(queue, plane, rows):
+    for q in range(4):
+        queue.dma_start(out=plane[32 * q : 32 * q + 4, :].bitcast(I32), in_=rows[4 * q : 4 * q + 4, :].bitcast(I32))
+
+
+def tile_list_rows_largerpicks_tabled_rowpeaks_kernel(
+    tc, xf, fk, w_words, w_scales, us, tg, wb_words, wb_scales, rs, offs, offs2, offs3, out
+):
+    nc = tc.nc
+    with ExitStack() as ctx:
+        sb = ctx.enter_context(tc.tile_pool(name="sb", bufs=1))
+        ps = ctx.enter_context(tc.psum_pool(name="ps", bufs=1))
+
+        def tile(shape, dtype, name, tag=None):
+            return sb.tile(shape, dtype, name=name, tag=tag or name, align_bytes=64)
+
+        list_a = tile([P, J // 16], U16, "list_a")
+        list_b = tile([P, J // 16], U16, "list_b")
+        list_g = tile([P, R // 16], U16, "list_g")
+        x = [tile([P, T], F32, "x%d" % t) for t in range(PACK)]
+        gates = [tile([P, C], F32, "gates%d" % h) for h in range(HALVES)]
+        fk_sb = tile([P, PACK], F32, "fk_sb")
+        us_sb = tile([P, PACK], F32, "us_sb")
+        w_raw = tile([P, 2 * R], U8, "w_raw")
+        w_sc_raw = tile([P, R], U8, "w_sc_raw")
+        ident = tile([P, P], F32, "ident")
+
+        nc.vector.memset(w_sc_raw[:].bitcast(U32), 0)
+        make_identity(nc, ident[:])
+        wb_sc = tile([P, N], U8, "wb_sc")
+        nc.gpsimd.memset(wb_sc[:].bitcast(U32), 0)
+
+        x_rows = xf.rearrange("(p t) c -> p t c", t=PACK)
+        nc.sync.dma_start(list_a[:], offs)
+        nc.sync.dma_start(list_b[:], offs2)
+        for t in range(PACK):
+            nc.sync.dma_start(out=x[t][:], in_=x_rows[:, t, :])
+        nc.sync.dma_start(out=fk_sb[:], in_=fk.rearrange("(p t) o -> p (t o)", t=PACK))
+        nc.sync.dma_start(list_g[:], offs3)
+        for h in range(HALVES):
+            nc.sync.dma_start(out=gates[h][:], in_=tg[h * P : (h + 1) * P, :])
+        nc.sync.dma_start(out=w_raw[:].bitcast(I32), in_=w_words[0].bitcast(I32))
+        load_scale_rows(nc.sync, w_sc_raw, w_scales[0])
+        nc.sync.dma_start(out=us_sb[:], in_=us.rearrange("o (p t) -> p (o t)", t=PACK))
+        load_scale_rows(nc.sync, wb_sc, wb_scales[0])
+
+        larger = tile([P, PACK, J], F32, "larger")
+        pick_a = tile([P, PACK, J], F32, "pick_a")
+        pick_b = tile([P, PACK, J], F32, "pick_b")
+        for t in range(PACK):
+            nc.scalar.activation(out=pick_a[:, t, :], in_=x[t][:].indirect(list_a[:]), func=ACT.Copy)
+            nc.vector.tensor_copy(out=pick_b[:, t, :], in_=x[t][:].indirect(list_b[:]))
+        nc.vector.tensor_tensor(out=larger[:], in0=pick_a[:], in1=pick_b[:], op=ALU.max)
+
+        res = tile([P, HALVES, N], F32, "res", tag="x0")
+        wb = tile([P, 2 * N], U8, "wb", tag="x1")
+        nc.sync.dma_start(out=res[:], in_=rs.rearrange("(h p) n -> p h n", p=P))
+        nc.sync.dma_start(out=wb[:].bitcast(I32), in_=wb_words[0].bitcast(I32))
+
+        sig = []
+        for h, reused in enumerate(("x3", "gates0")):
+            sig.append(tile([P, R], F32, "sig%d" % h, tag=reused))
+            nc.scalar.activation(out=sig[h][:], in_=gates[h][:].indirect(list_g[:]), func=ACT.Sigmoid)
+
+        u_bf = [tile([P, P * PACK], BF16, "u_bf%d" % h) for h in range(HALVES)]
+        u_q = [tile([P, P], U32, "u_q%d" % h) for h in range(HALVES)]
+        u_sc = [tile([P, P], U8, "u_sc%d" % h) for h in range(HALVES)]
+        fk_b = fk_sb[:].unsqueeze(1).unsqueeze(3).broadcast_to([P, P // RUN, PACK, RUN])
+        for h in range(HALVES):
+            nc.vector.tensor_tensor(
+                out=u_bf[h][:].rearrange("p (c i t) -> p c t i", i=RUN, t=PACK),
+                in0=larger[:, :, h * P : (h + 1) * P].rearrange("p t (c i) -> p c t i", i=RUN),
+                in1=fk_b,
+                op=ALU.mult,
+            )
+        gate_t = [tile([P, PACK, P], F32, "gate_t0", tag="gates1"), tile([P, PACK, P], F32, "gate_t1")]
+        hid_bf = [tile([P, P * PACK], BF16, "hid_bf%d" % h) for h in range(HALVES)]
+        hid_q = [tile([P, P], U32, "hid_q%d" % h) for h in range(HALVES)]
+        hid_sc = [tile([P, P], U8, "hid_sc%d" % h) for h in range(HALVES)]
+        size = [tile([P, N], F32, "size%d" % h) for h in range(HALVES)]
+        shifted = [tile([P, N], F32, "shifted%d" % h) for h in range(HALVES)]
+        den = [tile([P, 1], F32, "den%d" % h) for h in range(HALVES)]
+        rinv = [tile([P, 1], F32, "rinv%d" % h) for h in range(HALVES)]
+        y = [tile([P, N], F32, "y%d" % h) for h in range(HALVES)]
+        a_t = [ps.tile([P, PACK, P], F32, name="a_t%d" % h) for h in range(HALVES)]
+        prod = [ps.tile([P, N], F32, name="prod%d" % h) for h in range(HALVES)]
+        turned0 = ps.tile([P, PACK, P], F32, name="turned0")
+        turned1 = [ps.tile([P, 2, P], F32, name="turned1_%d" % b) for b in range(2)]
+
+        def first_product(h):
+            for t in range(PACK):
+                nc.tensor.matmul_mx(
+                    out=a_t[h][:, t, :],
+                    lhsT=w_dealt[:, 2 * P * t : 2 * P * (t + 1)].bitcast(E2M1),
+                    lhsT_scale=w_sc[:, P * t : P * (t + 1)],
+                    rhs=u_q[h][:].bitcast(E4M3),
+                    rhs_scale=u_sc[h][:],
+                    start=True,
+                    stop=True,
+                )
+
+        def hidden(h):
+            nc.vector.tensor_tensor(
+                out=hid_bf[h][:].rearrange("p (c i t) -> p c t i", i=RUN, t=PACK),
+                in0=a_t[h][:].rearrange("p t (c i) -> p c t i", i=RUN),
+                in1=gate_t[h][:].rearrange("p t (c i) -> p c t i", i=RUN),
+                op=ALU.mult,
+            )
+
+        def second_product(h):
+            nc.vector.quantize_mx(out=hid_q[h][:].bitcast(E5M2), scales=hid_sc[h][:], in_=hid_bf[h][:])
+            nc.tensor.matmul_mx(
+                out=prod[h][:],
+                lhsT=hid_q[h][:].bitcast(E5M2),
+                lhsT_scale=hid_sc[h][:],
+                rhs=wb[:].bitcast(E2M1),
+                rhs_scale=wb_sc[:],
+                start=True,
+                stop=True,
+            )
+            nc.scalar.activation(out=size[h][:], in_=prod[h][:], func=ACT.Abs)
+
+        def peak(h):
+            nc.vector.tensor_scalar(
+                out=shifted[h][:], in0=size[h][:], scalar1=0.2, scalar2=None, op0=ALU.add, op1=ALU.max, accum_out=den[h][:]
+            )
+            nc.vector.reciprocal(out=rinv[h][:], in_=den[h][:])
+
+        def finish(h):
+            nc.vector.scalar_tensor_tensor(
+                out=y[h][:], in0=prod[h][:], scalar=rinv[h][:], in1=res3[:, h, :], op0=ALU.mult, op1=ALU.add
+            )
+            nc.sync.dma_start(out=out[h * P : (h + 1) * P, :], in_=y[h][:])
+
+        for t in range(PACK):
+            nc.tensor.transpose(turned0[:, t, :], sig[0][:, t:R:PACK], ident[:])
+        w_dealt = tile([P, 2 * R], U8, "w_dealt", tag="x3")
+        w_sc = tile([P, R], U8, "w_sc", tag="fk_sb")
+        nc.vector.quantize_mx(out=u_q[0][:].bitcast(E4M3), scales=u_sc[0][:], in_=u_bf[0][:])
+        nc.vector.tensor_copy(
+            out=w_dealt[:].bitcast(U16).rearrange("p (t m) -> p t m", t=PACK),
+            in_=w_raw[:].bitcast(U16).rearrange("p (m t) -> p t m", t=PACK),
+        )
+        nc.vector.tensor_copy(
+            out=w_sc[:].rearrange("p (t m) -> p m t", t=PACK),
+            in_=w_sc_raw[:].rearrange("p (m t) -> p m t", t=PACK),
+        )
+        nc.vector.quantize_mx(out=u_q[1][:].bitcast(E4M3), scales=u_sc[1][:], in_=u_bf[1][:])
+
+        for t in range(PACK):
+            nc.scalar.activation(out=gate_t[0][:, t, :], in_=turned0[:, t, :], func=ACT.Copy, scale=us_sb[:, t : t + 1])
+        first_product(0)
+        for t in range(PACK):
+            nc.tensor.transpose(turned1[t // 2][:, t % 2, :], sig[1][:, t:R:PACK], ident[:])
+        for t in range(PACK):
+            nc.scalar.activation(
+                out=gate_t[1][:, t, :], in_=turned1[t // 2][:, t % 2, :], func=ACT.Copy, scale=us_sb[:, t : t + 1]
+            )
+        res3 = tile([P, HALVES, N], F32, "res3", tag="us_sb")
+        nc.scalar.activation(out=res3[:], in_=res[:], func=ACT.Copy, scale=0.3)
+        first_product(1)
+        hidden(0)
+        second_product(0)
+        hidden(1)
+        second_product(1)
+        peak(0)
+        finish(0)
+        peak(1)
+        finish(1)

@@ -56,6 +56,10 @@ def tile_list_rows_largerpicks_tabled_rowpeaks_kernel(
         wb_sc = tile([P, N], U8, "wb_sc")
         nc.gpsimd.memset(wb_sc[:].bitcast(U32), 0)
 
+        warm = tile([P, 2], F32, "warm")
+        nc.vector.memset(warm[:, 0:1], 0.0)
+        nc.scalar.activation(out=warm[:, 1:2], in_=warm[:, 0:1], func=ACT.Sigmoid)
+
         x_rows = xf.rearrange("(p t) c -> p t c", t=PACK)
         nc.sync.dma_start(list_a[:], offs)
         nc.sync.dma_start(list_b[:], offs2)

@@ -61,9 +61,10 @@ def tile_list_rows_largerpicks_tabled_rowpeaks_kernel(
         nc.scalar.activation(out=warm[:, 1:2], in_=warm[:, 0:1], func=ACT.Sigmoid)
 
         x_rows = xf.rearrange("(p t) c -> p t c", t=PACK)
+        nc.sync.dma_start(out=x[0][:], in_=x_rows[:, 0, :])
         nc.sync.dma_start(list_a[:], offs)
         nc.sync.dma_start(list_b[:], offs2)
-        for t in range(PACK):
+        for t in range(1, PACK):
             nc.sync.dma_start(out=x[t][:], in_=x_rows[:, t, :])
         nc.sync.dma_start(out=fk_sb[:], in_=fk.rearrange("(p t) o -> p (t o)", t=PACK))
         nc.sync.dma_start(list_g[:], offs3)
@@ -96,14 +97,29 @@ def tile_list_rows_largerpicks_tabled_rowpeaks_kernel(
         u_q = [tile([P, P], U32, "u_q%d" % h) for h in range(HALVES)]
         u_sc = [tile([P, P], U8, "u_sc%d" % h) for h in range(HALVES)]
         fk_b = fk_sb[:].unsqueeze(1).unsqueeze(3).broadcast_to([P, P // RUN, PACK, RUN])
-        for h in range(HALVES):
+
+        def scale_and_round(h):
             nc.vector.tensor_tensor(
                 out=u_bf[h][:].rearrange("p (c i t) -> p c t i", i=RUN, t=PACK),
                 in0=larger[:, :, h * P : (h + 1) * P].rearrange("p t (c i) -> p c t i", i=RUN),
                 in1=fk_b,
                 op=ALU.mult,
             )
-        gate_t = [tile([P, PACK, P], F32, "gate_t0", tag="gates1"), tile([P, PACK, P], F32, "gate_t1")]
+
+        scale_and_round(0)
+        w_dealt = tile([P, 2 * R], U8, "w_dealt", tag="pick_a")
+        w_sc = tile([P, R], U8, "w_sc", tag="pick_b")
+        nc.vector.tensor_copy(
+            out=w_dealt[:].bitcast(U16).rearrange("p (t m) -> p t m", t=PACK),
+            in_=w_raw[:].bitcast(U16).rearrange("p (m t) -> p t m", t=PACK),
+        )
+        nc.vector.tensor_copy(
+            out=w_sc[:].rearrange("p (t m) -> p m t", t=PACK),
+            in_=w_sc_raw[:].rearrange("p (m t) -> p m t", t=PACK),
+        )
+        nc.vector.quantize_mx(out=u_q[0][:].bitcast(E4M3), scales=u_sc[0][:], in_=u_bf[0][:])
+        scale_and_round(1)
+        gate_t = [tile([P, PACK, P], F32, "gate_t0", tag="larger"), tile([P, PACK, P], F32, "gate_t1")]
         hid_bf = [tile([P, P * PACK], BF16, "hid_bf%d" % h) for h in range(HALVES)]
         hid_q = [tile([P, P], U32, "hid_q%d" % h) for h in range(HALVES)]
         hid_sc = [tile([P, P], U8, "hid_sc%d" % h) for h in range(HALVES)]
@@ -164,21 +180,10 @@ def tile_list_rows_largerpicks_tabled_rowpeaks_kernel(
 
         for t in range(PACK):
             nc.tensor.transpose(turned0[:, t, :], sig[0][:, t:R:PACK], ident[:])
-        w_dealt = tile([P, 2 * R], U8, "w_dealt", tag="x3")
-        w_sc = tile([P, R], U8, "w_sc", tag="fk_sb")
-        nc.vector.quantize_mx(out=u_q[0][:].bitcast(E4M3), scales=u_sc[0][:], in_=u_bf[0][:])
-        nc.vector.tensor_copy(
-            out=w_dealt[:].bitcast(U16).rearrange("p (t m) -> p t m", t=PACK),
-            in_=w_raw[:].bitcast(U16).rearrange("p (m t) -> p t m", t=PACK),
-        )
-        nc.vector.tensor_copy(
-            out=w_sc[:].rearrange("p (t m) -> p m t", t=PACK),
-            in_=w_sc_raw[:].rearrange("p (m t) -> p m t", t=PACK),
+        nc.vector.tensor_tensor(
+            out=gate_t[0][:], in0=turned0[:], in1=us_sb[:].unsqueeze(2).broadcast_to([P, PACK, P]), op=ALU.mult
         )
         nc.vector.quantize_mx(out=u_q[1][:].bitcast(E4M3), scales=u_sc[1][:], in_=u_bf[1][:])
-
-        for t in range(PACK):
-            nc.scalar.activation(out=gate_t[0][:, t, :], in_=turned0[:, t, :], func=ACT.Copy, scale=us_sb[:, t : t + 1])
         first_product(0)
         for t in range(PACK):
             nc.tensor.transpose(turned1[t // 2][:, t % 2, :], sig[1][:, t:R:PACK], ident[:])

from contextlib import ExitStack

import concourse.mybir as mybir
from concourse.masks import make_identity

K, T, J, R, C, N = 512, 512, 256, 512, 1024, 256
FLOPS = 2 * K * J * R + 2 * R * J * N

F32 = mybir.dt.float32
BF16 = mybir.dt.bfloat16
I32 = mybir.dt.int32
U32 = mybir.dt.uint32
U16 = mybir.dt.uint16
U8 = mybir.dt.uint8
E4M3 = mybir.dt.float8_e4m3fn_x4
E5M2 = mybir.dt.float8_e5m2_x4
E2M1 = mybir.dt.float4_e2m1fn_x4
ALU = mybir.AluOpType
ACT = mybir.ActivationFunctionType

P = 128
PACK = 4
HALVES = J // P
RUN = 4


def load_scale_rows(queue, plane, rows):
    for q in range(4):
        queue.dma_start(out=plane[32 * q : 32 * q + 4, :].bitcast(I32), in_=rows[4 * q : 4 * q + 4, :].bitcast(I32))


def tile_list_rows_largerpicks_tabled_rowpeaks_kernel(
    tc, xf, fk, w_words, w_scales, us, tg, wb_words, wb_scales, rs, offs, offs2, offs3, out
):
    nc = tc.nc
    with ExitStack() as ctx:
        sb = ctx.enter_context(tc.tile_pool(name="sb", bufs=1))
        ps = ctx.enter_context(tc.psum_pool(name="ps", bufs=1))

        def tile(shape, dtype, name, tag=None):
            return sb.tile(shape, dtype, name=name, tag=tag or name, align_bytes=64)

        list_a = tile([P, J // 16], U16, "list_a")
        list_b = tile([P, J // 16], U16, "list_b")
        list_g = tile([P, R // 16], U16, "list_g")
        x = [tile([P, T], F32, "x%d" % t) for t in range(PACK)]
        gates = [tile([P, C], F32, "gates%d" % h) for h in range(HALVES)]
        fk_sb = tile([P, PACK], F32, "fk_sb")
        us_sb = tile([P, PACK], F32, "us_sb")
        w_raw = tile([P, 2 * R], U8, "w_raw")
        w_sc_raw = tile([P, R], U8, "w_sc_raw")
        ident = tile([P, P], F32, "ident")

        nc.vector.memset(w_sc_raw[:].bitcast(U32), 0)
        make_identity(nc, ident[:])
        wb_sc = tile([P, N], U8, "wb_sc")
        nc.gpsimd.memset(wb_sc[:].bitcast(U32), 0)

        warm = tile([P, 2], F32, "warm")
        nc.vector.memset(warm[:, 0:1], 0.0)
        nc.scalar.activation(out=warm[:, 1:2], in_=warm[:, 0:1], func=ACT.Sigmoid)

        x_rows = xf.rearrange("(p t) c -> p t c", t=PACK)
        nc.sync.dma_start(out=x[0][:], in_=x_rows[:, 0, :])
        nc.sync.dma_start(list_a[:], offs)
        nc.sync.dma_start(list_b[:], offs2)
        for t in range(1, PACK):
            nc.sync.dma_start(out=x[t][:], in_=x_rows[:, t, :])
        nc.sync.dma_start(out=fk_sb[:], in_=fk.rearrange("(p t) o -> p (t o)", t=PACK))
        nc.sync.dma_start(list_g[:], offs3)
        for h in range(HALVES):
            nc.sync.dma_start(out=gates[h][:], in_=tg[h * P : (h + 1) * P, :])
        nc.sync.dma_start(out=w_raw[:].bitcast(I32), in_=w_words[0].bitcast(I32))
        load_scale_rows(nc.sync, w_sc_raw, w_scales[0])
        nc.sync.dma_start(out=us_sb[:], in_=us.rearrange("o (p t) -> p (o t)", t=PACK))
        load_scale_rows(nc.sync, wb_sc, wb_scales[0])

        larger = tile([P, PACK, J], F32, "larger")
        pick_a = tile([P, PACK, J], F32, "pick_a")
        pick_b = tile([P, PACK, J], F32, "pick_b")
        for t in range(PACK):
            nc.scalar.activation(out=pick_a[:, t, :], in_=x[t][:].indirect(list_a[:]), func=ACT.Copy)
            nc.vector.tensor_copy(out=pick_b[:, t, :], in_=x[t][:].indirect(list_b[:]))
        nc.vector.tensor_tensor(out=larger[:], in0=pick_a[:], in1=pick_b[:], op=ALU.max)

        res = tile([P, HALVES, N], F32, "res", tag="x0")
        wb = tile([P, 2 * N], U8, "wb", tag="x1")
        nc.sync.dma_start(out=res[:], in_=rs.rearrange("(h p) n -> p h n", p=P))
        nc.sync.dma_start(out=wb[:].bitcast(I32), in_=wb_words[0].bitcast(I32))

        sig = []
        for h, reused in enumerate(("x3", "gates0")):
            sig.append(tile([P, R], F32, "sig%d" % h, tag=reused))
            nc.scalar.activation(out=sig[h][:], in_=gates[h][:].indirect(list_g[:]), func=ACT.Sigmoid)

        u_bf = [tile([P, P * PACK], BF16, "u_bf%d" % h) for h in range(HALVES)]
        u_q = [tile([P, P], U32, "u_q%d" % h) for h in range(HALVES)]
        u_sc = [tile([P, P], U8, "u_sc%d" % h) for h in range(HALVES)]
        fk_b = fk_sb[:].unsqueeze(1).unsqueeze(3).broadcast_to([P, P // RUN, PACK, RUN])

        def scale_and_round(h):
            nc.vector.tensor_tensor(
                out=u_bf[h][:].rearrange("p (c i t) -> p c t i", i=RUN, t=PACK),
                in0=larger[:, :, h * P : (h + 1) * P].rearrange("p t (c i) -> p c t i", i=RUN),
                in1=fk_b,
                op=ALU.mult,
            )

        scale_and_round(0)
        w_dealt = tile([P, 2 * R], U8, "w_dealt", tag="pick_a")
        w_sc = tile([P, R], U8, "w_sc", tag="pick_b")
        nc.vector.tensor_copy(
            out=w_dealt[:].bitcast(U16).rearrange("p (t m) -> p t m", t=PACK),
            in_=w_raw[:].bitcast(U16).rearrange("p (m t) -> p t m", t=PACK),
        )
        nc.vector.tensor_copy(
            out=w_sc[:].rearrange("p (t m) -> p m t", t=PACK),
            in_=w_sc_raw[:].rearrange("p (m t) -> p m t", t=PACK),
        )
        nc.vector.quantize_mx(out=u_q[0][:].bitcast(E4M3), scales=u_sc[0][:], in_=u_bf[0][:])
        scale_and_round(1)
        gate_t = [tile([P, PACK, P], F32, "gate_t0", tag="larger"), tile([P, PACK, P], F32, "gate_t1")]
        hid_bf = [tile([P, P * PACK], BF16, "hid_bf%d" % h) for h in range(HALVES)]
        hid_q = [tile([P, P], U32, "hid_q%d" % h) for h in range(HALVES)]
        hid_sc = [tile([P, P], U8, "hid_sc%d" % h) for h in range(HALVES)]
        size = [tile([P, N], F32, "size%d" % h) for h in range(HALVES)]
        shifted = [tile([P, N], F32, "shifted%d" % h) for h in range(HALVES)]
        den = [tile([P, 1], F32, "den%d" % h) for h in range(HALVES)]
        rinv = [tile([P, 1], F32, "rinv%d" % h) for h in range(HALVES)]
        y = [tile([P, N], F32, "y%d" % h) for h in range(HALVES)]
        a_t = [ps.tile([P, PACK, P], F32, name="a_t%d" % h) for h in range(HALVES)]
        prod = [ps.tile([P, N], F32, name="prod%d" % h) for h in range(HALVES)]
        turned0 = ps.tile([P, PACK, P], F32, name="turned0")
        turned1 = [ps.tile([P, 2, P], F32, name="turned1_%d" % b) for b in range(2)]

        def first_product(h):
            for t in range(PACK):
                nc.tensor.matmul_mx(
                    out=a_t[h][:, t, :],
                    lhsT=w_dealt[:, 2 * P * t : 2 * P * (t + 1)].bitcast(E2M1),
                    lhsT_scale=w_sc[:, P * t : P * (t + 1)],
                    rhs=u_q[h][:].bitcast(E4M3),
                    rhs_scale=u_sc[h][:],
                    start=True,
                    stop=True,
                )

        def hidden(h):
            nc.vector.tensor_tensor(
                out=hid_bf[h][:].rearrange("p (c i t) -> p c t i", i=RUN, t=PACK),
                in0=a_t[h][:].rearrange("p t (c i) -> p c t i", i=RUN),
                in1=gate_t[h][:].rearrange("p t (c i) -> p c t i", i=RUN),
                op=ALU.mult,
            )

        def second_product(h):
            nc.vector.quantize_mx(out=hid_q[h][:].bitcast(E5M2), scales=hid_sc[h][:], in_=hid_bf[h][:])
            nc.tensor.matmul_mx(
                out=prod[h][:],
                lhsT=hid_q[h][:].bitcast(E5M2),
                lhsT_scale=hid_sc[h][:],
                rhs=wb[:].bitcast(E2M1),
                rhs_scale=wb_sc[:],
                start=True,
                stop=True,
            )
            nc.scalar.activation(out=size[h][:], in_=prod[h][:], func=ACT.Abs)

        def peak(h):
            nc.vector.tensor_scalar(
                out=shifted[h][:], in0=size[h][:], scalar1=0.2, scalar2=None, op0=ALU.add, op1=ALU.max, accum_out=den[h][:]
            )
            nc.vector.reciprocal(out=rinv[h][:], in_=den[h][:])

        def finish(h):
            nc.vector.scalar_tensor_tensor(
                out=y[h][:], in0=prod[h][:], scalar=rinv[h][:], in1=res3[:, h, :], op0=ALU.mult, op1=ALU.add
            )
            nc.sync.dma_start(out=out[h * P : (h + 1) * P, :], in_=y[h][:])

        for t in range(PACK):
            nc.tensor.transpose(turned0[:, t, :], sig[0][:, t:R:PACK], ident[:])
        nc.vector.tensor_tensor(
            out=gate_t[0][:], in0=turned0[:], in1=us_sb[:].unsqueeze(2).broadcast_to([P, PACK, P]), op=ALU.mult
        )
        nc.vector.quantize_mx(out=u_q[1][:].bitcast(E4M3), scales=u_sc[1][:], in_=u_bf[1][:])
        first_product(0)
        for t in range(PACK):
            nc.tensor.transpose(turned1[t // 2][:, t % 2, :], sig[1][:, t:R:PACK], ident[:])
        for t in range(PACK):
            nc.scalar.activation(
                out=gate_t[1][:, t, :], in_=turned1[t // 2][:, t % 2, :], func=ACT.Copy, scale=us_sb[:, t : t + 1]
            )
        res3 = tile([P, HALVES, N], F32, "res3", tag="us_sb")
        nc.scalar.activation(out=res3[:], in_=res[:], func=ACT.Copy, scale=0.3)
        first_product(1)
        hidden(0)
        second_product(0)
        hidden(1)
        second_product(1)
        peak(0)
        finish(0)
        peak(1)
        finish(1)
